import numpy as np, ml_dtypes
CORES = [9,25,41,57]
N = 4
BF = ml_dtypes.bfloat16
def gentries(a):
    return np.ascontiguousarray(a.reshape(8, 16, -1).transpose(0, 2, 1)).reshape(8, -1)
def gtable(e):
    e = np.asarray(e); return np.ascontiguousarray(e.reshape(8, -1, 16).transpose(0, 2, 1)).reshape(128, -1).astype(np.int32)
V, H, I, L, R, CAP, MV, RO = 3072, 1024, 128, 2048, 2048, 192, 3, 3
Z = V + I * RO
W = Z + I * (RO - 1)
def grow(rng, few=0):
    S = H // 8; n = (V - H) // S
    lo = 0.1 + 0.25 * rng.random((N, 8, 1, S)); wd = 0.2 + 0.4 * rng.random((N, 8, 1, S)); sh = 1.5 * rng.standard_normal((N, 8, 16, S))
    def keys(pos):
        x = 15 * (lo[..., None] + wd[..., None] * pos) + sh[..., None] + 0.7 * rng.standard_normal((N, 8, 16, S, 8 + n), dtype=np.float32)
        x = np.clip(np.rint(x), 0, 15).astype(np.int64)
        return np.concatenate([x[..., :8].reshape(N, 8, 16, H), x[..., 8:].reshape(N, 8, 16, V - H)], axis=3)
    half = np.linspace(0.0, 1.0, 2 * n + 1)
    pa = np.concatenate([np.array([0.5, 0.25, 0.75, 0.1, 0.3, 0.5, 0.7, 0.9]), half[1::2]])
    pb = np.concatenate([np.array([1.0, 0.5, 1.0, 0.2, 0.4, 0.6, 0.8, 1.0]), half[2::2]])
    ids = np.concatenate([8 * np.arange(S)[:, None] + np.arange(8), H + n * np.arange(S)[:, None] + np.arange(n)], axis=1)
    kids = [[1, 3, 5] + [8 + 2 * i * n // 10 for i in range(5)], [2, 4, 6] + [8 + (2 * i + 1) * n // 10 for i in range(5)]]
    lk = [np.concatenate([ids[:, k].reshape(-1), np.zeros(V - H, np.int64)]) for k in kids]
    r = np.array([-1, 2, -1, 4, 5, 6, 7, -1] + list(range(9, 8 + n)) + [-1])
    lr = np.where(r >= 0, ids[:, r], -1); lr = np.concatenate([lr[:, :8].reshape(-1), lr[:, 8:].reshape(-1)])
    ph = np.concatenate([np.argsort(rng.random((N, 8, H)), axis=-1), H + np.argsort(rng.random((N, 8, V - H)), axis=-1)], axis=2); inv = np.argsort(ph, axis=-1)
    ka = np.take_along_axis(keys(pa), inv[:, :, None, :], 3); kb = np.take_along_axis(keys(pb), inv[:, :, None, :], 3)
    ca, cb = [np.where(np.arange(V) < H, np.take_along_axis(ph, k[inv], 2), rng.integers(0, R, (N, 8, V))) for k in lk]
    rr = lr[inv]; rt = np.where((rr >= 0) & (rng.random((N, 8, V)) < 0.94), np.take_along_axis(ph, np.maximum(rr, 0), 2), -1)
    it = np.where(rng.random((N, 8, 1, R)) < 0.5, rng.integers(0, 3, (N, 8, 16, R)), rng.integers(0, 16, (N, 8, 16, R)))
    if few:
        pool = 8 * rng.integers(0, S, (N, 8, few)) + rng.integers(3, 8, (N, 8, few)); s = np.take_along_axis(pool, rng.integers(0, few, (N, 8, L)), 2)
    else: s = rng.integers(0, H, (N, 8, L))
    g = s >> 3; top = rng.choice(np.array([1.05, 1.2, 1.5, 2.0]), (N, 8, 1)); top[0, 0] = 2.0; top[1, 0] = 1.05
    u = (top + 0.1) * rng.random((N, 8, L)) - 0.1
    x = 15 * (np.take_along_axis(lo[:, :, 0], g, 2) + np.take_along_axis(wd[:, :, 0], g, 2) * u)
    q = np.clip(np.rint(x[:, :, None] + np.take_along_axis(sh, g[:, :, None, :], 3) + 0.7 * rng.standard_normal((N, 8, 16, L), dtype=np.float32)), 0, 15).astype(np.int64)
    v = np.take_along_axis(ph, s, 2); w = rng.integers(0, 1024, (N, 8, 16))
    return ka, kb, ca, cb, rt, it, q, v, w
def pack(ka, kb, ca, cb, rt, it, q, v, w):
    return {"kk": (ka + 16 * kb).reshape(N, 128, V).astype(np.float32).astype(BF), "c0": ca.astype(np.int32), "c1": cb.astype(np.int32), "rt": rt.astype(np.int32),
            "rec": it.reshape(N, 128, R).astype(np.float32).astype(BF), "qs": q.reshape(N, 128, L).astype(np.float32).astype(BF),
            "v0": np.stack([gtable(a) for a in v]), "wt": w.reshape(N, 128, 1).astype(np.int32)}
def setup_inputs(rng):
    return pack(*grow(rng))
def setup_inputs_room(rng):
    ka, kb, ca, cb, rt, it, q, v, w = grow(rng)
    for a in range(N):
        for g in range(8):
            e = rng.permutation(H)[:8]; z = H + rng.permutation(V - H)[:8]
            ca[a, g, e] = z; cb[a, g, e] = z; rt[a, g, e] = -1; rt[a, g, z] = -1; kb[a, g][:, z] = np.minimum(kb[a, g][:, z], 14)
            n = int(rng.choice(np.array([0, 1, CAP - 1, CAP, CAP + 1, 2 * CAP])))
            if a == 0: n = (CAP, CAP + 1, 2 * CAP, CAP - 1, 1, 0, CAP, CAP + 1)[g]
            if a == 1: n = (CAP, CAP, CAP + 1, 2 * CAP, CAP, CAP, 0, 1)[g]
            o = rng.permutation(L)
            if g % 2 == 0: o = np.concatenate([np.array([0, L - 1]), o[(o > 0) & (o < L - 1)]])
            hot, cool = o[:n], o[n:]
            m = np.argsort(rng.random((16, n)), axis=0); q[a, g][:, hot] = np.where(m < rng.integers(9, 17, n), 15, rng.integers(0, 16, (16, n)))
            m = np.argsort(rng.random((16, L - n)), axis=0); q[a, g][:, cool] = np.where(m < rng.integers(8, 17, L - n), 0, q[a, g][:, cool])
            v[a, g, hot] = rng.choice(e, n)
    return pack(ka, kb, ca, cb, rt, it, q, v, w)
def setup_inputs_crowd(rng):
    ka, kb, ca, cb, rt, it, q, v, w = grow(rng, 6)
    for a in range(N):
        for g in (5, 6, 7):
            if g < 7 or a % 2 == 0:
                z = H + rng.permutation(V - H)[:H + 1]; kb[a, g] = 15; rt[a, g] = -1; ca[a, g, :H] = z[:H]; cb[a, g, :H] = z[:H]
            if g == 5: v[a, g, :I] = rng.permutation(H)[:I]
            if g == 6: v[a, g] = int(rng.integers(0, H))
            if g == 7 and a % 2 == 0:
                e = int(rng.integers(0, H // 4)); y = int(z[H]); ca[a, g, e] = y; cb[a, g, e] = y; kb[a, g, :, y] = rng.integers(0, 14, 16)
                hot = np.concatenate([np.array([0]), 1 + rng.permutation(L - 1)[:CAP - 1]])
                q[a, g][:, hot] = rng.integers(14, 16, (16, CAP)); q[a, g, :, 0] = 15; w[a, g] = 1023
                v[a, g] = rng.integers(H // 4, H, L); v[a, g, hot] = e
            if g == 7 and a % 2 == 1:
                o = rng.permutation(H)[:MV + 2]; y = int(rng.integers(H, V)); kb[a, g][:, o] = 0; kb[a, g, :, y] = 0
                rt[a, g, o[:-1]] = o[1:]; rt[a, g, o[-1]] = -1; rt[a, g, y] = -1; ca[a, g, o[-1]] = y; cb[a, g, o[-1]] = y
                v[a, g] = int(o[0]); q[a, g] = rng.integers(1, 16, (16, L))
    return pack(ka, kb, ca, cb, rt, it, q, v, w)
def setup_inputs_votes(rng):
    ka, kb, ca, cb, rt, it, q, v, w = grow(rng)
    base = rng.integers(2, 12, (N, 8, 16, 1)); kb = base + rng.integers(0, 2, (N, 8, 1, V)); ka = base - rng.integers(0, 2, (N, 8, 1, V))
    m = np.argsort(rng.random((N, 8, 16, L)), axis=2) < rng.choice(np.array([8, 9]), (N, 8, 1, L))
    q = np.where(m, base + 1 + rng.integers(0, 2, (N, 8, 1, L)), base - rng.integers(0, 2, (N, 8, 16, L)))
    it[..., ::2] = 0
    return pack(ka, kb, ca, cb, rt, it, q, v, w)
def setup_inputs_ends(rng):
    ka, kb, ca, cb, rt, it, q, v, w = grow(rng); inner = np.arange(V) < H
    for a in range(N):
        for g in range(8):
            if g % 4 == 0: rt[a, g] = -1
            if g % 4 == 1:
                o = rng.permutation(H); rt[a, g, o] = np.roll(o, -1); o = H + rng.permutation(V - H); rt[a, g, o] = np.roll(o, -1)
            if g % 4 == 2:
                e = np.array([0, H - 1, H, V - 1]); z = np.array([0, R - 1])
                ca[a, g] = np.where(inner, rng.choice(e, V), rng.choice(z, V)); cb[a, g] = np.where(inner, rng.choice(e, V), rng.choice(z, V))
            if g % 4 == 3: rt[a, g] = np.where(rng.random(V) < 0.3, np.arange(V), rt[a, g])
    v[:, :, 0] = 0; v[:, :, L - 1] = H - 1
    return pack(ka, kb, ca, cb, rt, it, q, v, w)
def setup_inputs_spread(rng):
    inner = np.arange(V) < H
    def some(n):
        return np.minimum((16 * rng.random((N, 8, 16, n)) ** rng.choice(np.array([0.4, 1.0, 2.0, 4.0]), (N, 8, 1, n))).astype(np.int64), 15)
    ka, kb, q, it = some(V), some(V), some(L), some(R)
    ca = np.where(inner, rng.integers(0, V, (N, 8, V)), rng.integers(0, R, (N, 8, V))); cb = np.where(inner, rng.integers(0, V, (N, 8, V)), rng.integers(0, R, (N, 8, V)))
    rt = np.where(inner, rng.integers(0, H, (N, 8, V)), rng.integers(H, V, (N, 8, V))); rt = np.where(rng.random((N, 8, V)) < rng.choice(np.array([0.05, 0.2, 0.5]), (N, 8, 1)), -1, rt)
    v = rng.integers(0, H, (N, 8, L))
    for a in range(N):
        for g in range(8):
            o = 1 + rng.permutation(H - 1)[:2]; e = int(o[0]); u = 0 if g % 2 == 0 else int(o[1])
            o = H + rng.permutation(V - H)[:2]; z = int(o[0]); y = int(o[1])
            v[a, g, 0] = e; v[a, g, 1] = u; q[a, g, :, :2] = 0
            kb[a, g, :, e] = 0; ka[a, g, :, z] = np.maximum(ka[a, g, :, z], 1); rt[a, g, e] = u; ca[a, g, e] = z; cb[a, g, e] = z
            ka[a, g, :, u] = 0; kb[a, g, :, u] = 15; ka[a, g, :, y] = 0; ca[a, g, u] = y; cb[a, g, u] = z
    return pack(ka, kb, ca, cb, rt, it, q, v, rng.integers(0, 1024, (N, 8, 16)))
def check_inputs(d):
    bad = []
    for k, hi in (("kk", 255), ("rec", 15), ("qs", 15), ("v0", H - 1), ("wt", 1023)):
        x = np.asarray(d[k]).astype(np.float64)
        if not np.all((x >= 0) & (x <= hi) & (x == np.floor(x))): bad.append("range of " + k)
    for k in ("c0", "c1"):
        x = np.asarray(d[k]).astype(np.int64)
        if not (np.all((x[..., :H] >= 0) & (x[..., :H] < V)) and np.all((x[..., H:] >= 0) & (x[..., H:] < R))): bad.append("range of " + k)
    x = np.asarray(d["rt"]).astype(np.int64); y = x[..., H:]
    if not (np.all((x[..., :H] >= -1) & (x[..., :H] < H)) and np.all((y == -1) | ((y >= H) & (y < V)))): bad.append("range of rt")
    return bad
def above(a, b):
    return np.sum(a > b, axis=2) >= 9
def pick(t, ix):
    return np.take_along_axis(t, ix[:, :, None, :] if t.ndim == 4 else ix, -1)
def lowest(ok, u):
    i = np.arange(u.shape[2]); key = np.where(ok, u, W + i)
    return ok & ~np.any((key[..., :, None] == key[..., None, :]) & (i[None, :] < i[:, None]), axis=3)
def insert(ka, kb, ca, cb, gr, win, n, m, p, cn, new):
    a, e, i = np.nonzero(win); n = n[a, e, i]; m = m[a, e, :, i]; p = p[a, e, i]; cn = cn[a, e, i]; x = new[i]
    k0 = ka[a, e, :, n]; k1 = kb[a, e, :, n]; b = np.sum(m > k0, axis=1) >= 9
    o0 = np.where(b, ca[a, e, n], cn); o1 = np.where(b, cn, cb[a, e, n])
    ka[a, e, :, x] = k1; kb[a, e, :, x] = k1; ca[a, e, x] = o1; cb[a, e, x] = o1; gr[a, e, x] = gr[a, e, n]; gr[a, e, n] = x
    kb[a, e, :, n] = np.where(b[:, None], m, k0); ka[a, e, :, n] = np.where(b[:, None], k0, m)
    cb[a, e, n] = np.where(b, p, o0); ca[a, e, n] = np.where(b, o0, p)
def reference(kk, c0, c1, rt, rec, qs, v0, wt):
    k = kk.astype(np.float32).astype(np.int16).reshape(N, 8, 16, V)
    ka = np.zeros((N, 8, 16, W), np.int16); kb = np.zeros((N, 8, 16, W), np.int16); ka[..., :V] = k & 15; kb[..., :V] = k >> 4
    ca = np.zeros((N, 8, W), np.int64); cb = np.zeros((N, 8, W), np.int64); gr = np.zeros((N, 8, W), np.int64)
    ca[..., :V] = c0; cb[..., :V] = c1; gr[..., :V] = rt
    it = rec.astype(np.float32).astype(np.int16).reshape(N, 8, 16, R); q = qs.astype(np.float32).astype(np.int16).reshape(N, 8, 16, L)
    wg = wt.astype(np.int64).reshape(N, 8, 16); v = np.stack([gentries(a) for a in v0]).astype(np.int64); fi = np.array(v)
    pon = np.zeros((N, 8, I), bool); pv = np.zeros((N, 8, I), np.int64); pf = np.zeros((N, 8, I), np.int64); lane = np.arange(I)
    for t in range(RO):
        for step in range(MV + 1):
            hi = above(q, pick(kb, v)); b = above(q, pick(ka, v)); g = pick(gr, v); c = np.where(b, pick(cb, v), pick(ca, v)); leaf = (v >= H) & (v < Z)
            if step == MV: break
            right = hi & (g >= 0); down = ~right & ~leaf
            fi = np.where(down, v, fi); v = np.where(right, g, np.where(down, c, v))
        done = leaf & ~hi; over = hi & (g < 0)
        if t > 0:
            m = pick(kb, pv); gu = pick(gr, pf); u = np.where(above(m, pick(kb, pf)) & (gu >= 0), gu, pf)
            cu = np.where(above(m, pick(ka, u)), pick(cb, u), pick(ca, u)); ok = pon & (cu == pv)
            insert(ka, kb, ca, cb, gr, lowest(ok, u), u, m, pv, np.broadcast_to(V + I * (t - 1) + lane, pv.shape), Z + I * (t - 1) + lane)
        pv = np.array(v[:, :, :I]); pf = np.array(fi[:, :, :I]); pon = lowest(done[:, :, :I], pv)
        insert(ka, kb, ca, cb, gr, pon, pv, q[..., :I], c[:, :, :I], c[:, :, :I], V + I * t + lane)
        q = np.where(done[:, :, None, :], (q + pick(it, np.where(done, c, 0)) + t) & 15, q).astype(np.int16); v = np.where(done, fi, v)
        before = np.add.accumulate(over.astype(np.int64), axis=2) - over
        a, e, l = np.nonzero(over & (before < CAP)); s = before[a, e, l]
        box = np.zeros((N, 8, 16, CAP), np.int16); have = np.zeros((N, 8, CAP), bool); box[a, e, :, s] = q[a, e, :, l]; have[a, e, s] = True
        src = (a - 1) % N; nq = np.where(have[src, e, s][:, None], box[src, e, :, s], q[a, e, :, l])
        q[a, e, :, l] = nq; st = np.sum(nq.astype(np.int64) * wg[a, e], axis=1) & (H - 1); v[a, e, l] = st; fi[a, e, l] = st
    return {"yk": (ka + 16 * kb).reshape(N, 128, W).astype(np.float32).astype(BF), "y0": ca.astype(np.float32), "y1": cb.astype(np.float32), "yr": gr.astype(np.float32),
            "yq": q.reshape(N, 128, L).astype(np.float32).astype(BF)}

from concourse.mybir import AluOpType as ALU, ActivationFunctionType as AF

V, H, I, L, R, CAP, RO = 3072, 1024, 128, 2048, 2048, 192, 3
Z = V + I * RO
W = Z + I * (RO - 1)
WX = W + I
TV = 288
SG, HS = (1, 1), (1, 1)
KEYS = (9.5, 8.5, 8.9, 8.0, 1.0)
SEED, NOISE, SPAN, PASSES = 3, 1200.0, 20000.0, 700
BF, F3, I3, U2 = "bfloat16", "float32", "int32", "uint16"
MATS = ["ZERO", "ID", "IDn", "ID16", "ID32", "ID17", "DIN", "BSKi", "BIN", "BSELF", "BSELFn", "BC0", "BCd", "BSKo", "UB", "D10", "D6", "D13",
        "LA0", "LA1", "LA2", "LB", "LX0", "LX1", "LX2", "LK1", "LK2", "LPa", "LPb", "LPc", "LY1", "LY2", "LYb", "LYc", "TM", "IOT", "NEG"]
BUF = [("KK", WX, BF), ("TK", WX, F3), ("PT", WX, BF), ("IT", R + 16, BF), ("q0", L + CAP, BF), ("q1", L + CAP, BF), ("QX", L, F3),
       ("HH", V, BF), ("SS", L, BF), ("RR", L, BF), ("AA", L, BF), ("PG", L, BF), ("vi", 128, I3), ("VL", 128, U2), ("PL", 128, U2),
       ("ci", 768, I3), ("XX", 4096, BF), ("zz", 128, F3), ("xf", 256, F3), ("x3", 128, F3),
       ("BO", 640, BF), ("WB", 40, BF), ("WP", 6 * 32, BF), ("WL", 48, BF), ("WY", 112, BF),
       ("Z1", 144, BF), ("ZB", 144, BF), ("ZR", 144, BF), ("ZH", 144, BF), ("ZL", 144, BF), ("Z12", 112, BF),
       ("SF", 128, F3), ("SB", 128, BF), ("SO", 128, BF), ("col", 16, F3), ("coi", 8, I3), ("wi", 1, I3), ("wh", 1, BF),
       ("I256", 256, BF), ("SLL", 256, BF), ("TMf", 128, F3), ("JR", 192, BF), ("JB", 16, F3), ("JD", 16, F3), ("DM", 8, F3), ("DM16", 8, F3),
       ("JI", 8, I3), ("JL", 8, U2), ("ONE", 128, F3),
       ("ovL", 128, BF), ("Pin", 128, F3), ("lin", 128, F3), ("acc", 12, F3), ("cf", 12, F3), ("c16", 12, F3),
       ("CL", 12, U2), ("BB", 192, BF), ("lane", 12, F3), ("lanx", 12, F3), ("LL", 12, U2), ("XG", 12, U2), ("SND", 3 * 208, BF), ("LND", 3 * 208, BF),
       ("sl", 128, BF), ("nsl", 128, BF), ("vp", 128, F3), ("hi", 128, I3), ("ef", 8, F3), ("EL", 8, U2), ("YO", 928, F3),
       ("M16", 128, BF), ("ui", 8, I3), ("UL", 8, U2), ("bt", 128, BF), ("Pe", 128, BF), ("Pu", 128, BF), ("uz", 128, BF), ("ok", 128, BF)]
for _p in "ip":
    for _n, _c, _d in [("b", 128, BF), ("kB", 128, F3), ("kB2", 128, F3), ("kL", 8, F3), ("nf", 8, F3), ("t8", 8, F3), ("dv", 8, F3), ("ED", 128, BF),
                       ("EE", 7 * 128, BF), ("win", 128, BF), ("TG", 8, U2), ("kv", 128, BF), ("hv", 128, BF), ("tt", 128, BF),
                       ("M", 128, BF), ("KV", 128, BF), ("TW", 128, F3), ("u", 128, BF), ("PV", 128, BF)]:
        BUF.append((_p + _n, _c, _d))
SCRATCH, AT, KIND = {}, {}, {}
_fill = {}
for _n, _c, _d in BUF:
    KIND[_n] = ("sbuf", _c, _d)
    if _c <= 192 and _n not in ("vi", "wi"):
        AT[_n] = ("pool_" + _d, _fill.get(_d, 0))
        _fill[_d] = _fill.get(_d, 0) + (_c + 15) // 16 * 16
    else:
        AT[_n] = (_n, 0)
        SCRATCH[_n] = ("sbuf", [128, _c], _d)
for _d in _fill:
    SCRATCH["pool_" + _d] = ("sbuf", [128, _fill[_d]], _d)
SCRATCH["CM"] = ("sbuf", [128, 8 * len(MATS), 16], BF)
KIND["CM"] = ("sbuf", 0, BF)
PADS = ("XP0", "XP1", "XQ0", "XQ1", "XE", "YP0", "YP1", "YQ0", "YQ1", "YE", "OP0", "OP1")
for _n in PADS:
    SCRATCH[_n] = ("sbuf", [128, 17, 8], F3 if _n[0] == "X" else BF)
    KIND[_n] = ("sbuf", 136, SCRATCH[_n][2])
for _k in range(8):
    SCRATCH["ps%d" % _k] = ("psum", [128, 512], F3)
    KIND["ps%d" % _k] = ("psum", 512, F3)
    AT["ps%d" % _k] = ("ps%d" % _k, 0)
SEMAPHORES = ["cv", "cs", "ct", "cg", "sent", "arr0", "arr1", "arr2"] + ["d%d" % _k for _k in range(32)]
CYC, PEC, GAT, SCA, LAT = 1.04, 0.52, 1.56, 3.8, 70.0
PLAN = {}


def rank_program(g, core, T, topo):
    rank = T.rank_of(core)
    if rank is None:
        return
    n_ranks = len(T.cores)
    nxt = T.cores[(rank + 1) % n_ranks]
    prv = T.cores[(rank - 1) % n_ranks]
    Q = {"v": g.vector, "s": g.scalar, "t": g.tensor, "g": g, "y": g.sync}
    ops = []
    key = [-2.0]

    def A(n, a=0, b=None, st=1, p=(0, 128)):
        if b is None:
            b = KIND[n][1]
        r, o = AT[n]
        x = T[r][p[0]:p[1], o + a:o + b:st] if st > 1 else T[r][p[0]:p[1], o + a:o + b]
        return (x, [(n, a, b)], (b - a + st - 1) // st, n)

    def PADW(n, p=128):
        return (T[n][0:p, 1:17:2, :], [(n, 0, 136)], 64, n)

    def PADR(n, k, p=128):
        return (T[n][0:p, 1 - k:17 - k, :], [(n, 0, 136)], 128, n)

    def IND(w, o):
        return (w[0].indirect(o[0]), w[1], o[2] * 16, w[3], o[1])

    def M(n, b=0, w=16, p=128):
        k = MATS.index(n)
        return (T.CM[0:p, 8 * k:8 * k + p // 16, b:b + w], [("CM", k, k + 1)], p // 16 * w, "CM")

    def C(k, p=(0, 128)):
        return A("col", k, k + 1, 1, p)

    def two(x):
        return KIND[x[3]][2] in (BF, U2)

    def psum(x):
        return KIND[x[3]][0] == "psum"

    def ap(x):
        return x[0] if isinstance(x, tuple) else x

    def add(e, fn, out, ins, cost, lat=0.0, sem=None, more=()):
        rd = []
        for x in ins:
            if isinstance(x, tuple):
                rd += x[1] + (x[4] if len(x) > 4 else [])
        wr = []
        for x in ([out] if out else []) + list(more):
            wr += x[1]
            rd += x[4] if len(x) > 4 else []
        ops.append({"e": e, "fn": fn, "rd": rd, "wr": wr, "c": cost, "lat": lat, "sem": sem, "k": key[0]})

    def vcost(out, a, w):
        if len(out) > 4:
            return 50 + out[2] * SCA * CYC
        if len(a) > 4:
            return 60 + out[2] * GAT * CYC
        return 40 + max(64, out[2] * w) * CYC

    def cp(out, a):
        add("v", lambda: g.vector.tensor_copy(out[0], a[0]), out, [a], vcost(out, a, 0.5 if two(out) and two(a) else 1))

    def tt(out, a, b, op):
        add("v", lambda: g.vector.tensor_tensor(out[0], a[0], b[0], op), out, [a, b], vcost(out, a, 1 if psum(a) or psum(b) else 2))

    def ts(out, a, s1, o1, s2=None, o2=None):
        if s2 is None:
            fn = lambda: g.vector.tensor_scalar(out[0], a[0], ap(s1), None, o1)
        else:
            fn = lambda: g.vector.tensor_scalar(out[0], a[0], ap(s1), ap(s2), o1, o2)
        add("v", fn, out, [a, s1, s2], vcost(out, a, 0.5 if two(out) and two(a) else 1))

    def ms(out, c):
        add("v", lambda: g.vector.memset(out[0], c), out, [], vcost(out, out, 0.5 if two(out) else 1))

    def act(out, a, scale=1.0, bias=0.0, f=AF.Identity, acc=None):
        if acc is None:
            fn = lambda: g.scalar.activation(out[0], a[0], f, bias=ap(bias), scale=ap(scale))
        else:
            fn = lambda: g.scalar.activation(out[0], a[0], f, bias=ap(bias), scale=ap(scale), accum_out=acc[0])
        add("s", fn, out, [a, scale, bias], vcost(out, a, 1) + (20 if acc else 0), more=[acc] if acc else [])

    def mm(out, l, r, start=True, stop=True):
        add("t", lambda: g.tensor.matmul(out[0], l[0], r[0], start, stop), out, [l, r],
            max(64, out[2]) * (1 if two(l) else 4) * PEC)

    def mms(out, pairs):
        for k, (l, r) in enumerate(pairs):
            mm(out, l, r, k == 0, k == len(pairs) - 1)

    def iota(out, pat, base, cm):
        if KIND[out[3]][2] == I3:
            fn = lambda: g.iota(out[0], pat, base, cm)
        else:
            fn = lambda: g.iota(out[0], pat, base, cm, allow_small_or_imprecise_dtypes=True)
        add("g", fn, out, [], 130 + 2 * out[2] * CYC)

    def sel(out, a, pat, op, fill, base, cm):
        add("g", lambda: g.affine_select(out[0], a[0], pat, op, fill, base, cm), out, [a], 170 + 2 * out[2] * CYC)

    nd = [0]

    def dma(e, o, i, wr, rd, nbytes, slow=False):
        s = "d%d" % nd[0]
        nd[0] += 1
        if slow:
            fn = lambda: g.dma_start(o, i, allow_slow_non_contiguous=True)
        else:
            fn = lambda: Q[e].dma_start(o, i)
        add(e, fn, wr, [rd] if rd else [], 60 if e != "g" else 1000, 2000 + nbytes / 250.0, (s, 16))

    def band(x, n, inner):
        pat = ([[0, n]] if n > 1 else [])
        sel(x, x, pat + [[-16, 8]] + inner, ALU.is_ge, 0.0, 0, 1)
        sel(x, x, pat + [[16, 8]] + inner, ALU.is_ge, 0.0, 15, -1)

    def ent(x, a, c):
        sel(x, x, [[-16, 8]], ALU.not_equal, float(c), -a, 1)

    def pmat(n, es, src="ZERO"):
        a, b, c, w = es[0]
        sel(M(n), M(src), [[-16, 8], [1000, 16]], ALU.not_equal, float(c), -a - 1000 * b, 1)
        for a, b, c, w in es[1:]:
            sel(M(n, b, w), M(n, b, w), [[-16, 8], [-1, w]], ALU.not_equal, float(c), -a, 1)

    def rmat(n, es):
        src = "ZERO"
        for a, c in es:
            sel(M(n), M(src), [[-16, 8], [0, 16]], ALU.not_equal, float(c), -a, 1)
            src = n

    NIL = (0, 0, 0, 1)

    def load(e, n, a, b, src, p=(0, 128), slow=False):
        x = A(n, a, b, 1, p)
        dma(e, x[0], src, x, None, (p[1] - p[0]) * (b - a) * (2 if two(x) else 4), slow)

    P96 = (0, 96)
    for k, x in enumerate((T.c0, T.c1, T.rt)):
        load("s", "ci", 256 * k, 256 * k + 256, x[:], P96)
    for k in range(2):
        load("y", "KK", 1536 * k, 1536 * k + 1536, T.kk[:, 1536 * k:1536 * k + 1536])
    load("y", "q0", 0, L, T.qs[:])
    load("y", "vi", 0, 128, T.v0[:])
    load("y", "IT", 0, R, T.rec[:])
    load("g", "wi", 0, 1, T.wt[:], slow=True)

    ms(M("ZERO"), 0.0)
    iota(C(0), [[0, 1]], 0, 1)
    cp(A("coi", 0, 1), C(0))
    ts(A("coi", 1, 2), A("coi", 0, 1), 15, ALU.bitwise_and)
    cp(C(1), A("coi", 1, 2))
    tt(C(2), C(0), C(1), ALU.subtract)
    ts(C(11), C(1), 7.5, ALU.is_lt, 6144.0, ALU.mult)
    ts(C(3), C(11), -3096.0, ALU.add)
    ts(C(4), C(11), -1.0, ALU.mult, 5143.5, ALU.add)
    ts(A("coi", 2, 3), C(0), 1.0 / 12, ALU.mult, -0.45, ALU.add)
    ts(C(5), A("coi", 2, 3), -12.0, ALU.mult, C(0), ALU.add)
    ts(C(6), C(5), 3.5, ALU.is_lt)
    ts(C(7), C(5), 3.5, ALU.is_gt)
    ts(C(8), C(5), 256.0, ALU.mult)
    ts(C(9), C(8), C(7), ALU.mult)
    ts(C(10), C(6), 4096.0, ALU.mult)
    sel(M("ID"), M("ZERO"), [[-1, 128]], ALU.not_equal, 1.0, 0, 1)
    ms(A("Z12"), 0.0)
    ms(A("Z12", 11, 107, 12), 1.0)
    band(A("Z12", 11, 107, 12), 1, [])
    iota(A("I256"), [[1, 256]], 0, 0)
    for k, c in enumerate((-512.0, 131072.0, -131072.0, 65536.0, -16384.0)):
        ms(A("WB", 8 * k, 8 * k + 8), c)
    band(A("WB"), 5, [])
    iota(A("WP", 0, 32), [[0, 32]], 0, 0)
    for f, rows in enumerate(((4, 5, 6), (7, 8), (12, 13, 14), (9, 10, 11))):
        for a in rows:
            ent(A("WP", 8 * f, 8 * f + 8), a, 1)
    for k in range(1, 6):
        sel(A("WP", 32 * k, 32 * k + 32), A("WP", 0, 32), [[1000, 4], [-16, 8]], ALU.not_equal, float(k + 1), -14 - 2000, 1)
    ms(A("SF"), 0.0)
    for n, c, src in (("SF", 1.0, A("SF")), ("SB", -4096.0, M("ZERO")), ("SO", 1.0, M("ZERO"))):
        sel(A(n), src, [[-1, 2], [-2, 64]], ALU.not_equal, c, 0, 1)
    for n in PADS:
        iota((T[n][:], [(n, 0, 136)], 136, n), [[0, 136]], 0, 0)
    iota(A("xf"), [[0, 256]], 0, 0)
    key[0] = KEYS[4]
    for n, c in (("IDn", -1), ("ID16", 16), ("ID32", 32), ("ID17", 17.0 / 16)):
        sel(M(n), M("ZERO"), [[-1, 128]], ALU.not_equal, float(c), 0, 1)
    iota(A("WL"), [[0, 48]], 0, 0)
    for f, es in enumerate((((2, 1), (3, 1), (4, 1)), ((0, 1), (1, 1)), ((14, 1024), (15, -62)), ((14, -1024), (15, 64)), ((11, -1),), ((12, 1), (13, 1)))):
        for a, c in es:
            ent(A("WL", 8 * f, 8 * f + 8), a, c)
    iota(A("BO", 0, 128), [[0, 128]], 1, 0)
    band(A("BO", 0, 128), 1, [[0, 16]])
    BO = [A("BO", 128 * k, 128 * k + 128) for k in range(5)]
    for k, c in enumerate((-1.0 / 16, -2.0, 64.0, -512.0)):
        act(BO[k + 1], BO[0], c)
    sel(M("UB"), BO[0], [[-1, 128]], ALU.is_gt, 0.0, 0, 1)
    iota(A("Z1"), [[0, 144]], 0, 0)
    iota(A("Z1", 15, 143, 16), [[0, 8]], 1, 0)
    band(A("Z1", 15, 143, 16), 1, [])
    act(A("ZB"), A("Z1"), 131072.0)
    iota(A("ZR"), [[0, 144]], 0, 0)
    for a in (9, 10, 11):
        ent(A("ZR", 15, 143, 16), a, 1)
    cp(C(12), A("wi"))
    cp(A("wh"), C(12))
    tt(C(13), C(12), A("wh"), ALU.subtract)
    ts(A("ZH"), A("Z1"), A("wh"), ALU.mult)
    ts(A("ZL"), A("Z1"), C(13), ALU.mult)
    iota(M("IOT"), [[1, 128]], 0, 0)
    iota(M("NEG"), [[0, 128]], -2064, 0)
    iota(A("TMf"), [[0, 8], [-1, 16]], 0, 1)
    ts(M("TM"), A("TMf"), C(2), ALU.is_ge, 8192.0, ALU.mult)
    iota(A("JR"), [[1, 192]], 0, 0)
    iota(A("JD"), [[16, 16]], 0, 0)
    ts(A("JB"), A("JD"), C(1), ALU.add, 0.5, ALU.add)
    act(A("DM"), A("JB", 0, 8), 1.0, W - 0.5)
    act(A("DM16"), A("DM"), 16.0)
    act(A("JD"), A("JB"), 1.0, L - 0.5)
    iota(A("JI"), [[1, 8]], 0, 0)
    cp(A("JL"), A("JI"))
    iota(A("ONE"), [[0, 128]], 1, 0)
    for n in ("q0", "q1"):
        iota(A(n, L, L + CAP), [[0, CAP]], 0, 0)
    for n in ("KK", "TK", "PT"):
        iota(A(n, Z - I, Z), [[0, I]], 0, 0)
    rmat("BSKi", [(4, 2.0 ** -13)])
    rmat("BIN", [(14, 1.0 / 64)])
    rmat("BSELF", [(12, 1), (13, 1)])
    sel(M("BSKo"), BO[0], [[0, 8], [1, 16]], ALU.is_equal, 0.0, -4, 0)
    act(M("BSKo"), M("BSKo"), 16384.0)
    pmat("D10", [(10, 10, 1, 1)])
    pmat("D6", [(6, 6, 1, 1), (8, 8, 1, 1), (13, 13, 1, 1)])
    pmat("LB", [NIL, (0, 2, -1, 2), (2, 2, 1, 2)])
    pmat("LA0", [(15, 9, V / 1024, 1), (15, 11, -64, 1), (0, 0, 1, 2), (5, 5, 1, 4), (12, 12, 1, 4), (0, 2, 1, 2)])
    pmat("LX0", [(15, b, V / 1024, 1) for b in (5, 7, 12)] + [(2, 2, 1, 3), (9, 9, 1, 3), (14, 14, 1, 2), (2, 0, 1, 2)])
    for t in (1, 2):
        pmat("LA%d" % t, [(15, 9, (V + I * t) / 1024, 1)], "LA0")
        pmat("LX%d" % t, [(15, b, (V + I * t) / 1024, 1) for b in (5, 7, 12)], "LX0")
    act(M("BSELFn"), M("BSELF"), -1.0)
    rmat("BC0", [(0, 1), (1, 1)])
    rmat("BCd", [(0, -1), (1, -1), (2, 1), (3, 1)])
    pmat("D13", [(13, 13, 1, 1)])
    pmat("LK1", [(15, 9, Z / 1024, 1), (15, 11, -64, 1), (12, 12, 1, 4)])
    pmat("LK2", [(15, 9, (Z + I) / 1024, 1)], "LK1")
    pmat("LPa", [NIL, (12, 0, 1, 2), (12, 7, 1, 2), (9, 2, 1, 2), (9, 5, 1, 2)])
    pmat("LPb", [NIL, (12, 0, -1, 2), (12, 7, -1, 2), (9, 2, -1, 2), (9, 5, -1, 2), (12, 2, 1, 2), (12, 5, 1, 2)])
    pmat("LPc", [NIL, (0, 0, 1, 2), (0, 7, 1, 2)])
    pmat("LY1", [(15, 12, Z / 1024, 1), (2, 0, 1, 2), (2, 5, 1, 2), (2, 7, 1, 2), (2, 2, 1, 3), (9, 9, 1, 3), (14, 14, 1, 2)])
    pmat("LY2", [(15, 12, (Z + I) / 1024, 1)], "LY1")
    pmat("LYb", [NIL] + [(2, b, -1, 2) for b in (0, 2, 5, 7)])
    pmat("LYc", [NIL] + [(9, b, 1, 2) for b in (0, 2, 5, 7)])
    iota(A("WY"), [[0, 112]], 0, 0)
    for f, a in enumerate((0, 2, 9)):
        for d in (0, 1):
            ent(A("WY", 3 + 32 * f, 35 + 32 * f, 4), a + d, 1)

    key[0] = -1.5

    def X(a):
        return A("XX", 256 * a, 256 * a + 256, 1, P96)
    for k, a in enumerate((0, 2, 9)):
        c = A("ci", 256 * k, 256 * k + 256, 1, P96)
        ts(X(a), c, 0.0, ALU.add)
        tt(X(a + 1), c, X(a), ALU.subtract)
    i256 = A("I256", 0, 256, 1, P96)
    ts(M("DIN"), M("ID"), C(6), ALU.mult)
    act(A("SLL", 0, 256, 1, P96), i256, C(7, P96))
    for a, b in ((2, 5), (0, 7)):
        act(X(b), X(a), C(6, P96), C(9, P96))
        bank = A("ps7", 128 * a, 128 * a + 256, 1, P96)
        mms(bank, [(M("DIN", 0, 16, 96), X(a + 1)), (M("ID", 0, 16, 96), A("SLL", 0, 256, 1, P96))])
        act(X(b + 1), bank)
    ts(X(11), A("ci", 512, 768, 1, P96), 0.0, ALU.is_lt, -2.0 ** 22, ALU.mult)
    act(X(11), X(11), 1.0, -65536.0)
    act(X(12), i256, 0.0, C(8, P96))
    iota(X(13), [[1, 256]], 0, 0)
    act(X(14), i256, 0.0, C(10, P96))
    iota(X(15), [[0, 256]], 1024, 0)
    for k in range(6):
        ts(A("HH", 512 * k, 512 * k + 512), A("KK", 512 * k, 512 * k + 512), 2056.5, ALU.add)
    mms(A("ps6", 0, 256, 1, P96), [(A("Z12", 11 - j, 107 - j), A("HH", 256 * j, 256 * j + 256)) for j in range(12)])
    act(X(4), A("ps6", 0, 256, 1, P96), 1024.0, -2064.0 * 16384)
    for j in range(12):
        dma("y", T.PT[:, 256 * j:256 * j + 256], T.XX[j:96:12, :], A("PT", 256 * j, 256 * j + 256), A("XX"), 65536)
    key[0] = -1.0
    for k in range(6):
        a, b = 512 * k, 512 * k + 512
        bank = A("ps%d" % (4 + k % 2))
        mms(bank, [(M("ID"), A("KK", a, b)), (M("ID"), A("HH", a, b))])
        if k % 2:
            cp(A("TK", a, b), bank)
        else:
            act(A("TK", a, b), bank)
    cp(A("VL"), A("vi"))

    def lanes(n, h, s):
        return A(n, 1024 * h + s, 1024 * h + 1024, 8)

    def half(n, h):
        return A(n, 64 * h, 64 * h + 64)

    def prep(q, h):
        a = 1024 * h
        act(A("QX", a, a + 1024), A(q, a, a + 1024), 33.0, C(4))
        for s in range(8):
            mm(A("ps%d" % h, 384 + s, 448, 8), lanes(q, h, s), A("WB", 32, 40))
        act(half("zz", h), A("ps%d" % h, 384, 448), 1.0, -69632.0)

    def turn(out, xp, yp, p=128, n=64):
        pp = (0, p)
        mms(out, [(PADR(xp, k, p), A("SF", 64 * k, 64 * k + n, 1, pp)) for k in range(2)] + [(PADR(yp, k, p), A("SB", 64 * k, 64 * k + n, 1, pp)) for k in range(2)])

    def votes(h, win, wp, nf, na, fa, wide, n0):
        a = 1024 * h
        y = "ps%d" % h
        c = 64 * h + TV // 16
        key[0] = n0
        tt(A("RR", a + TV, a + 1024), IND(A("TK", 0, win), A("VL", c, 64 * h + 64)), A("QX", a + TV, a + 1024), ALU.subtract)
        act(A("PG", a, a + 1024), IND(A("PT", 0, win), half("VL", h)))
        key[0] = n0 + 0.3
        tt(A("RR", a, a + TV), IND(A("TK", 0, win), A("VL", 64 * h, c)), A("QX", a, a + TV), ALU.subtract)
        key[0] = n0 + 0.5
        act(A("AA", a + TV, a + 1024), A("RR", a + TV, a + 1024), -1.0, C(3), AF.Sign)
        ts(A("AA", a, a + TV), A("RR", a, a + TV), C(3), ALU.is_lt, 0.5, ALU.subtract)
        key[0] = n0 + 0.8
        mm(A(y, 0, 64 * nf), M("ZERO"), A("IT", 0, 64 * nf), True, False)
        for s in range(8):
            mm(A(y, s, 64 * nf, 8), lanes("PG", h, s), wp, False, False)
        for s in range(8):
            mm(A(y, s, 64, 8), lanes("RR", h, s), A("WB", 0, 8), False, False)
        for s in range(8):
            mm(A(y, 64 * fa + s, 64 * (fa + na), 8), lanes("AA", h, s), A("WB", 8, 8 + 8 * na), False, s == 7)
        key[0] = n0 + 1.1
        x = A("xf", 128 * h, 128 * h + 64)
        tt(x, A(y, 0, 64), half("zz", h), ALU.add)
        tt(A("xf", 128 * h, 128 * h + wide), A(y, 64, 64 + wide), A("xf", 128 * h, 128 * h + wide), ALU.max)
        tt(PADW("XP%d" % h), A(y, 64 * fa, 64 * fa + 64), x, ALU.max)
        key[0] = n0 + 1.4
        act(PADW("YP%d" % h), PADW("XP%d" % h), 1.0 / 4096, 143.55)
        turn(A("ps%d" % (2 + h), 0, 64), "XP%d" % h, "YP%d" % h)
        key[0] = n0 + 1.7

    def to_list(out, zb, src, n, first=True, last=True):
        for s in range(16):
            mm(out, A(zb, 15 - s, 143 - s), A(src[3], src[1][0][1] + s, src[1][0][1] + 16 * n, 16), first and s == 0, last and s == 15)

    def lowest(x, src, extra, bound):
        mms(A("ps6", 128, 256), [(M("BSELF"), src)])
        mms(A("ps6", 256, 384), [(M("BSELF"), src), (M("ID"), M("TM"))])
        act(A(x + "kB"), A("ps6", 128, 256))
        act(A(x + "kB2"), A("ps6", 256, 384))
        tt(A(x + "ED"), IND(A(x + "kL"), A("JL")), A(x + "kB2"), ALU.is_equal)
        for j in range(7):
            ts(A(x + "EE", 144 * j + 16, 128 * j + 128), A(x + "kB", 16 * j + 16, 128), A(x + "kL", j, j + 1), ALU.is_equal)
        mm(A("ps6", 384, 512), BO[3], A(x + "ED"), True, False)
        for j in range(7):
            mm(A("ps6", 400 + 16 * j, 512), BO[3], A(x + "EE", 144 * j + 16, 128 * j + 128), False, False)
        for k, (l, r) in enumerate(extra):
            mm(A("ps6", 384, 512), l, r, False, k == len(extra) - 1)
        ts(A(x + "win"), A("ps6", 384, 512), bound, ALU.is_lt)
        to_list(A("ps7", 0, 8), "Z1", A(x + "win"), 8)
        tt(A(x + "dv"), A(x + "nf"), A("DM"), ALU.subtract)
        tt(A(x + "t8"), A("ps7", 0, 8), A(x + "dv"), ALU.mult)
        tt(A(x + "t8"), A(x + "t8"), A("DM16"), ALU.add)
        ts(A(x + "TG"), A(x + "t8"), 1.0 / 16, ALU.mult)

    def oldkeys(x, lst, win, m):
        act(A(x + "kv"), IND(A("KK", 0, win), lst))
        act(A(x + "hv"), A(x + "kv"), 1.0, 2056.5)
        mms(A("ps7", 128, 256), [(M("ID"), m), (M("IDn"), A(x + "kv")), (M("ID"), A(x + "hv")), (M("ID"), M("NEG"))])

    def newkeys(x, m, tk):
        mms(A("ps7", 256, 384), [(M("ID"), A(x + "kv")), (M("IDn"), A(x + "hv")), (M("ID"), A(x + "tt"))])
        act(A(x + "M"), A("ps7", 256, 384), 1.0, 2064.0)
        mms(A("ps7", 384, 512), [(M("ID"), m), (M("IDn"), A(x + "tt")), (M("ID16"), A(x + "M"))])
        act(A(x + "KV"), A("ps7", 384, 512))
        if tk:
            mms(A("ps7", 256, 384), [(M("ID"), m), (M("IDn"), A(x + "tt")), (M("ID32"), A(x + "M"))])
            act(A(x + "TW"), A("ps7", 256, 384), 1.0, 2064.0)

    def made(x, base, pairs, tk):
        mms(A("ps6", 0, 128), pairs)
        mms(A("ps6", 128, 256), [(M("ID17"), A(x + "hv")), (M("ID17"), M("NEG"))])
        tt(A("PT", base, base + I), A("ps6", 0, 128), A(x + "win"), ALU.mult)
        tt(A("KK", base, base + I), A("ps6", 128, 256), A(x + "win"), ALU.mult)
        if tk:
            act(A("TK", base, base + I), A(x + "hv"), 33.0 / 16, 2064.0 - 33 * 129)

    def scatter(x, tk):
        if tk:
            cp(IND(A("TK"), A(x + "TG")), A(x + "TW"))
        cp(IND(A("PT"), A(x + "TG")), A(x + "PV"))
        cp(IND(A("KK"), A(x + "TG")), A(x + "KV"))

    for h in range(2):
        prep("q0", h)
    rid, pid = topo.addr(nxt)[:2]
    emask = topo.mask(core, nxt)
    n_out = len(topo.engines(core, nxt))
    n_in = len(topo.engines(prv, core))
    for t in range(RO):
        last = t == RO - 1
        q, qn = "q%d" % (t % 2), "q%d" % (1 - t % 2)
        win = (V, V + I, Z + I)[t]
        key[0] = 10 * t + KEYS[0]
        if t > 0:
            tt(A("bt"), IND(A("KK", 0, win), A("EL")), A("M16"), ALU.is_lt)
            act(A("Pe"), IND(A("PT", 0, win), A("EL")))
            to_list(A("ps7", 0, 8), "ZB", A("bt"), 8, True, False)
            to_list(A("ps7", 0, 8), "ZR", A("Pe"), 8, False, True)
            act(A("pt8"), A("ps7", 0, 8), 1.0, -8.0 * 131072)
            tt(A("ui"), A("pt8"), A("ef"), ALU.max)
            ts(A("ui"), A("ui"), 4095, ALU.bitwise_and)
            cp(A("UL"), A("ui"))
            cp(A("pnf"), A("ui"))
            act(A("Pu"), IND(A("PT", 0, win), A("UL")))
            oldkeys("p", A("UL"), win, A("iM"))
            ts(A("bt"), A("ps7", 128, 256), 0.5, ALU.is_gt)
            mms(A("ps6", 0, 128), [(BO[0], A("bt"))])
            ts(A("pb"), A("ps6", 0, 128), 8.5, ALU.is_gt)
            tt(A("ptt"), A("ps7", 128, 256), A("pb"), ALU.mult)
            mm(A("ps6", 128, 256), M("ID"), A("Pu"))
            mm(A("ps6", 256, 384), M("ID"), A("iPV"))
            tt(A("pu"), A("ps6", 128, 256), A("pb"), ALU.mult)
            tt(A("uz"), A("ps6", 256, 384), A("pb"), ALU.mult)
            mms(A("ps6", 0, 128), [(M("BC0"), A("Pu")), (M("BCd"), A("pu")), (M("BSELFn"), A("iPV")), (BO[4], A("iwin"))])
            ts(A("ok"), A("ps6", 0, 128), -8192.0, ALU.is_equal)
            to_list(A("ps7", 0, 8), "Z1", A("ok"), 8)
            act(A("pt8"), A("ps7", 0, 8), 512.0, -8192.0)
            tt(A("pkL"), A("pt8"), A("pnf"), ALU.add)
            newkeys("p", A("iM"), not last)
            mms(A("ps7", 128, 256), [(M("LK%d" % t), A("Pu")), (M("LPa"), A("iPV")), (M("LPb"), A("uz")), (M("LPc"), A("pu")),
                                     (M("BSKo"), A("pM")), (M("D10"), M("IOT"))])
            act(A("pPV"), A("ps7", 128, 256))
            lowest("p", A("Pu"), [(M("IDn"), A("ok"))], -0.5)
            made("p", Z + I * (t - 1), [(M("LY%d" % t), A("Pu")), (M("LYb"), A("pu")), (M("LYc"), A("uz")), (M("D13"), M("IOT"))], not last)
        for mv in range(3):
            k = 0 if last else 3 * t + mv
            for h in range(2):
                votes(h, win, A("WP", 32 * k, 32 * k + 32), 4, 1, 3, 64 if last else 128, 10 * t + 2 * mv + h)
                ts(half("VL", h), A("ps%d" % (2 + h), 0, 64), 589824.0, ALU.add)
        iota(A("IT", R, R + 16), [[0, 16]], -t, 0)
        for h in range(2):
            y = "ps%d" % h
            votes(h, win, A("WL"), 6, 3, 2, 64, 10 * t + 6 + h)
            ts(half("PL", h), A("ps%d" % (2 + h), 0, 64), 589824.0, ALU.add)
            ts(PADW("OP%d" % h), A(y, 256, 320), 65.5 * 65536, ALU.is_gt)
            mms(A("ps%d" % (2 + h), 64, 128), [(PADR("OP%d" % h, k), A("SO", 64 * k, 64 * k + 64)) for k in range(2)])
            act(half("ovL", h), A("ps%d" % (2 + h), 64, 128))
            if not last:
                ts(half("x3", h), A(y, 192, 256), 65536.0, ALU.min)
                tt(half("x3", h), half("x3", h), A("xf", 128 * h + 64, 128 * h + 128), ALU.add)
                tt(PADW("XQ%d" % h), A(y, 320, 384), half("x3", h), ALU.max)
                act(PADW("YQ%d" % h), PADW("XQ%d" % h), 1.0 / 4096, 143.55)
                turn(A("ps%d" % (4 + h), 0, 64), "XQ%d" % h, "YQ%d" % h)
                act(half("vp", h), A("ps%d" % (4 + h), 0, 64), 1.0, 589824.0 + 2.0 ** 19)
        key[0] = 10 * t + KEYS[3]
        mms(A("ps3", 256, 384), [(BO[0], A("ovL"))])
        mms(A("ps3", 384, 512), [(M("UB"), A("ovL"))])
        add("v", lambda: g.vector.tensor_tensor_scan(A("Pin")[0], A("ONE")[0], T.ps3[:, 256:384], 0.0, ALU.mult, ALU.add), A("Pin"), [A("ONE"), A("ps3", 256, 384)], 180)
        tt(A("lin"), A("Pin"), A("ps3", 384, 512), ALU.subtract)
        for j in range(12):
            act(A("HH", L + 128 * (j % 8), L + 128 * (j % 8) + 128), A("Pin"), -1.0, A("JB", j, j + 1), AF.Sign, A("acc", j, j + 1))
        act(A("cf"), A("acc"), 0.5, 64.0)
        ts(A("CL"), A("cf"), 127.0, ALU.min)
        ts(A("c16"), A("cf"), 127.0, ALU.min, 16.0, ALU.mult)
        tt(A("BB"), IND(A("lin"), A("CL")), A("JR"), ALU.is_le)
        to_list(A("ps2", 256, 268), "Z1", A("BB"), 12)
        tt(A("lane"), A("ps2", 256, 268), A("c16"), ALU.add)
        cp(A("LL"), A("lane"))
        o = 208 * t
        ts(A("SND", o + 192, o + 204), A("lane"), L - 0.5, ALU.is_gt)
        act(A("SND", o, o + 192), IND(A(q), A("LL")))
        add("g", lambda o=o, t=t: g.remote_dma(T.LND[:, o:o + 204], T.SND[:, o:o + 204], T.sem["arr%d" % t], T.sem.sent, pid, rid, emask),
            A("LND", o, o + 204), [A("SND", o, o + 204)], 1000, 2500, ("arr%d" % t, n_in))
        tt(A("lanx"), A("SND", o + 192, o + 204), A("JD", 0, 12), ALU.mult)
        tt(A("lanx"), A("lanx"), A("lane"), ALU.max)
        if not last:
            ts(A("nsl"), A("lin"), CAP + 0.5, ALU.is_lt, 2.0 ** 20, ALU.mult)
            tt(A("sl"), A("nsl"), A("ovL"), ALU.mult)
        key[0] = 10 * t + KEYS[1]
        pg, q1 = A("PG", 0, I), A(q, 0, I)
        mms(A("ps6", 0, 128), [(M("BSKi"), pg), (BO[1], A("RR", 0, I)), (BO[2], q1)])
        ts(A("ib"), A("ps6", 0, 128), 8.5, ALU.is_gt)
        cp(A("inf"), A("VL", 0, 8))
        ts(A("it8"), A("PL", 0, 8), R - 0.5, ALU.is_gt, 8192.0, ALU.mult)
        tt(A("ikL"), A("inf"), A("it8"), ALU.subtract)
        oldkeys("i", A("VL", 0, 8), win, q1)
        tt(A("itt"), A("ps7", 128, 256), A("ib"), ALU.mult)
        mm(A("ps6", 128, 256), M("ID"), pg)
        tt(A("iu"), A("ps6", 128, 256), A("ib"), ALU.mult)
        newkeys("i", q1, not last)
        mms(A("ps7", 128, 256), [(M("LA%d" % t), pg), (M("LB"), A("iu")), (M("BSKo"), A("iM")), (M("D10"), M("IOT"))])
        act(A("iPV"), A("ps7", 128, 256))
        lowest("i", pg, [(BO[0], A("AA", 0, I)), (M("BIN"), pg)], 0.25)
        if t > 0:
            scatter("p", not last)
        made("i", V + I * t, [(M("LX%d" % t), pg), (M("D6"), M("IOT"))], not last)
        scatter("i", not last)
        if not last:
            act(A("M16"), A("iM"), 16.0)
            act(PADW("XE", 16), A("xf", 64, 128, 1, (0, 16)))
            act(PADW("YE", 16), PADW("XE", 16), 1.0 / 4096, 143.55)
            turn(A("ps7", 0, 8), "XE", "YE", 16, 8)
            act(A("ef"), A("ps7", 0, 8), 1.0, 589824.0)
            cp(A("EL"), A("ef"))
        key[0] = 10 * t + KEYS[2]
        for h in range(2):
            for k in range(2):
                a = 1024 * h + 512 * k
                b = a + 512
                bank = A("ps%d" % (4 + k))
                item = IND(A("IT"), A("PL", a // 16, b // 16))
                own = [(M("ID"), A("SS", a, b))]
                src = A("SS", a, b)
                if SG[h] > k:
                    act(src, item)
                    own.append((M("ID"), A(q, a, b)))
                    mms(bank, own)
                    src = bank
                else:
                    tt(src, item, A(q, a, b), ALU.add)
                if HS[h] > k:
                    act(A("HH", a, b), src, 1.0, 2056.5 + t)
                else:
                    ts(A("HH", a, b), src, 2056.5 + t, ALU.add)
                mms(bank, own + [(M("IDn"), A("HH", a, b))])
                act(A(qn, a, b), bank, 1.0, 2064.0 + t)
        tt(A("cf"), A("LND", o + 192, o + 204), A("JD", 0, 12), ALU.mult)
        tt(A("cf"), A("cf"), A("lanx"), ALU.max)
        cp(A("XG"), A("cf"))
        cp(IND(A(qn), A("XG")), A("LND", o, o + 192))
        if not last:
            for h in range(2):
                hb = A("ps%d" % (2 + h), 192, 256)
                to_list(hb, "ZH", A(qn, 1024 * h, 1024 * h + 1024), 64, True, False)
                to_list(hb, "ZL", A(qn, 1024 * h, 1024 * h + 1024), 64, False, False)
                mm(hb, M("ID"), half("sl", h), False, True)
                prep(qn, h)
                cp(half("hi", h), hb)
                ts(half("hi", h), half("hi", h), 2 ** 20 + H - 1, ALU.bitwise_and)
                tt(half("hi", h), half("hi", h), half("vp", h), ALU.max)
                ts(half("hi", h), half("hi", h), 4095, ALU.bitwise_and)
                cp(half("VL", h), half("hi", h))
    key[0] = 40.0
    qn = "q%d" % (RO % 2)
    dma("y", T.yq[:], T[qn][:, 0:L], None, A(qn, 0, L), 524288)
    for k in range(2):
        dma("y", T.yk[:, 1856 * k:1856 * k + 1856], T.KK[:, 1856 * k:1856 * k + 1856], None, A("KK", 1856 * k, 1856 * k + 1856), 475136)
    for k in range(2):
        bank = A("ps%d" % k, 0, 464, 1, P96)
        mms(bank, [(A("WY", 3 - j, 99 - j), A("PT", 928 * j + 464 * k, 928 * j + 464 * k + 464)) for j in range(4)])
        if k:
            act(A("YO", 464, 928, 1, P96), bank)
        else:
            cp(A("YO", 0, 464, 1, P96), bank)
    for f, x in enumerate((T.y0, T.y1, T.yr)):
        dma("s" if f else "y", x[:], T.YO[32 * f:32 * f + 32, :], None, A("YO"), 118784)

    n = len(ops)
    pred = [dict() for _ in range(n)]
    hist = {}
    for i, op in enumerate(ops):
        for regs, w in ((op["rd"], False), (op["wr"], True)):
            for (b, lo, hi) in regs:
                bank = KIND[b][0] == "psum"
                for (j, l2, h2, w2) in hist.get(b, []):
                    same = ops[j]["e"] == op["e"] and ops[j]["sem"] is None and op["sem"] is None
                    if bank:
                        pred[i][j] = pred[i].get(j, False) or not same
                    elif l2 < hi and lo < h2 and (w or w2):
                        pred[i][j] = pred[i].get(j, False) or not same or w2
        for regs, w in ((op["rd"], False), (op["wr"], True)):
            for (b, lo, hi) in regs:
                old = hist.get(b, [])
                if KIND[b][0] == "psum":
                    old = []
                elif w:
                    old = [x for x in old if not (lo <= x[1] and x[2] <= hi)]
                hist[b] = old + [(i, lo, hi, w)]
    succ = [[] for _ in range(n)]
    for i in range(n):
        for j in pred[i]:
            succ[j].append(i)

    def lay(seq, before, back):
        beg = [0.0] * n
        busy = {e: [] for e in Q}
        for i in seq:
            t0 = 0.0
            for j in before[i]:
                a, b = (i, j) if back else (j, i)
                t0 = max(t0, beg[j] + ops[j]["c"] + ops[a]["lat"] + (LAT if pred[b][a] else 0.0))
            c = ops[i]["c"]
            if back and not before[i]:
                t0 = ops[i]["lat"]
            lst = busy[ops[i]["e"]]
            x = len(lst)
            while x > 0 and lst[x - 1][1] > t0:
                x -= 1
            while x < len(lst) and lst[x][0] < t0 + c:
                t0 = max(t0, lst[x][1])
                x += 1
            lst.insert(x, (t0, t0 + c))
            beg[i] = t0
        return beg, max(beg[i] + ops[i]["c"] + (0.0 if back else ops[i]["lat"]) for i in range(n))

    if "seq" not in PLAN:
        rnd = [SEED * 7919 + 1]

        def topo_order(val, noise):
            eff = []
            lo = 0.0
            if noise:
                rnd[0] = (rnd[0] * 1103515245 + 12345) % 2147483648
                lo = best[0] * rnd[0] / 2147483648.0 - SPAN / 2
            for i in range(n):
                rnd[0] = (rnd[0] * 1103515245 + 12345) % 2147483648
                eff.append(val[i] + (noise * (rnd[0] / 2147483648.0) if lo < val[i] < lo + SPAN else 0.0))
            for i in range(n - 1, -1, -1):
                for k in succ[i]:
                    eff[i] = min(eff[i], eff[k])
            return sorted(range(n), key=lambda i: (eff[i], i))
        best = None
        seq = topo_order([2500.0 * op["k"] for op in ops], 0.0)
        for x in range(PASSES):
            for _ in range(2 if x else 6):
                beg, end = lay(seq, pred, False)
                if best is None or end <= best[0]:
                    best = (end, beg)
                seq = sorted(range(n), key=lambda i: (-beg[i] - ops[i]["c"], -i))
                beg, end = lay(seq, succ, True)
                seq = topo_order([-beg[i] - ops[i]["c"] for i in range(n)], 0.0)
            seq = topo_order(best[1], NOISE)
        PLAN["seq"] = sorted(range(n), key=lambda i: (best[1][i], i))
        PLAN["end"] = best[0]
    order = {e: [i for i in PLAN["seq"] if ops[i]["e"] == e] for e in Q}
    place = {}
    for e in Q:
        for x, i in enumerate(order[e]):
            place[i] = x
    need = [[] for _ in range(n)]
    marked = set()
    for e in Q:
        seen = {}
        for i in order[e]:
            want = {}
            for j, tie in pred[i].items():
                if tie:
                    k = ops[j]["sem"][0] if ops[j]["sem"] else ops[j]["e"]
                    if k not in want or place[j] > place[want[k]]:
                        want[k] = j
            for k, j in want.items():
                if seen.get(k, -1) < place[j]:
                    seen[k] = place[j]
                    need[i].append(j)
                    marked.add(j)
    count = {}
    for e in Q:
        c = 0
        for i in order[e]:
            if ops[i]["sem"] is None and i in marked:
                c += 1
                count[i] = c
    for e in Q:
        for i in order[e]:
            for j in need[i]:
                if ops[j]["sem"]:
                    Q[e].wait_ge(T.sem[ops[j]["sem"][0]], ops[j]["sem"][1])
                else:
                    Q[e].wait_ge(T.sem["c" + ops[j]["e"]], count[j])
            ins = ops[i]["fn"]()
            if ops[i]["sem"]:
                if ops[i]["sem"][0][0] == "d":
                    ins.then_inc(T.sem[ops[i]["sem"][0]], 16)
            elif i in marked:
                ins.then_inc(T.sem["c" + e], 1)
    for i in range(n):
        if ops[i]["sem"] and i not in marked:
            g.sync.wait_ge(T.sem[ops[i]["sem"][0]], ops[i]["sem"][1])
    g.wait_ge(T.sem.sent, RO * n_out)
